import numpy as np
import ml_dtypes


def mxq(x, axis, fmt="e4m3"):
    dtype, down = {"e4m3": (ml_dtypes.float8_e4m3fn, 7), "e5m2": (ml_dtypes.float8_e5m2, 14)}[fmt]
    v = np.moveaxis(np.asarray(x, np.float32).astype(ml_dtypes.bfloat16).astype(np.float64), axis, -1)
    blocks = v.reshape(v.shape[:-1] + (-1, 32))
    amax = np.abs(blocks).max(-1, keepdims=True)
    byte = np.maximum(np.where(amax > 0, np.frexp(amax)[1] - 1 + 127, 0) - down, 1)
    scale = np.exp2(byte - 127.0)
    codes = (blocks / scale).astype(np.float32).astype(dtype).astype(np.float64)
    return np.moveaxis((codes * scale).reshape(v.shape), -1, axis)


WIDE = False


def mx_kscale(k):
    if not WIDE:
        return np.ones(k)
    levels = np.array([10, -10, 5, -5, 0])
    if k % 512:
        return np.exp2(np.random.permutation(np.resize(levels, k // 32))).repeat(32)
    a = np.empty((k // 512, 16))
    for p in range(k // 512):
        a[p, :8] = np.random.permutation(np.resize(levels, 8))
        for g in range(8):
            far = levels[np.abs(levels - a[p, g]) >= 10]
            a[p, g + 8] = far[np.random.randint(len(far))]
    return np.exp2(a.ravel()).repeat(32)


def f64(x):
    return np.asarray(x).astype(np.float64)


def striped(idx):
    return np.tile(idx.reshape(-1, 16).T, (8, 1)).astype(np.uint16)


def unstriped(offs):
    return offs[:16].T.reshape(-1).astype(np.int64)


E2M1 = np.array([0.0, 0.5, 1.0, 1.5, 2.0, 3.0, 4.0, 6.0, -0.0, -0.5, -1.0, -1.5, -2.0, -3.0, -4.0, -6.0])


def pack_weight(w, fmt):
    k, n = w.shape
    w = f64(np.asarray(w, np.float32).astype(ml_dtypes.bfloat16)).reshape(k // 32, 32, n)
    amax = np.abs(w).max(1)
    if fmt == "e4m3":
        byte = np.frexp(amax)[1] - 1 + 127 - 7
    else:
        mant, ex = np.frexp(amax / 6.0)
        byte = np.where(mant > 0.5, ex, ex - 1) + 127
    byte = np.clip(np.where(amax > 0, byte, 1), 1, 254)
    scaled = (w * np.exp2(127.0 - byte)[:, None, :]).reshape(k, n).astype(np.float32)
    by_word = np.ascontiguousarray(scaled.reshape(k // 512, 128, 4, n).transpose(0, 1, 3, 2))
    if fmt == "e4m3":
        words = by_word.astype(ml_dtypes.float8_e4m3fn).view(np.uint8)
    else:
        c = by_word.astype(ml_dtypes.float4_e2m1fn).view(np.uint8) & 0xF
        words = (c[..., 0::2] | (c[..., 1::2] << 4)).reshape(k // 512, 128, 2 * n)
    return np.ascontiguousarray(words), np.ascontiguousarray(byte.astype(np.uint8).reshape(k // 512, 16, n))


def unpack_weight(words, scales, fmt):
    g, _, n = scales.shape
    words = np.ascontiguousarray(words).reshape(g, 128, n, -1)
    if fmt == "e4m3":
        vals = words.view(ml_dtypes.float8_e4m3fn).astype(np.float64)
    else:
        nib = np.empty((g, 128, n, 4), np.uint8)
        nib[..., 0::2] = words & 0xF
        nib[..., 1::2] = words >> 4
        vals = E2M1[nib]
    vals = vals * np.repeat(np.exp2(scales.astype(np.float64) - 127.0), 8, axis=1)[..., None]
    return vals.transpose(0, 1, 3, 2).reshape(g * 512, n)


def gelu(v):
    return 0.5 * v * (1.0 + np.tanh(np.sqrt(2.0 / np.pi) * (v + 0.044715 * v**3)))


K, T, S, H, T2, P, N = 1024, 2048, 1024, 512, 2048, 1024, 384

def setup_inputs():
    n = np.random.standard_normal
    s = mx_kscale(K)[:, None]
    u = mx_kscale(H)[:, None]
    tab_words, tab_scales = pack_weight(n((K, T)) * s, "e4m3")
    w2_words, w2_scales = pack_weight(n((K, H)) / np.sqrt(K) / s, "e2m1")
    w4_words, w4_scales = pack_weight(n((H, N)) / np.sqrt(H) / u, "e4m3")
    return {
        "tab_words": tab_words, "tab_scales": tab_scales,
        "offs": striped(np.random.permutation(T)[:S]),
        "offs2": striped(np.random.permutation(T2)[:S]),
        "offs3": striped(np.random.permutation(T2)[:P]),
        "offs4": striped(np.random.permutation(T2)[:P]),
        "w1": (n((K, H)) * np.exp(0.6 * n(H)) / np.sqrt(K) / s).astype(np.float32),
        "w2_words": w2_words, "w2_scales": w2_scales,
        "gain": (1.5 * np.exp(0.2 * n(H)) * u[:, 0]).astype(np.float32),
        "wgs": np.exp(0.3 * n((128, S))).astype(np.float32),
        "page0": (0.8 * n((H, T2)) * u).astype(np.float32),
        "w3": (1.2 * n((K, N)) / np.sqrt(K) / s).astype(np.float32),
        "w4_words": w4_words, "w4_scales": w4_scales,
        "bias": (0.6 * n(N)).astype(np.float32),
    }

def reference(tab_words, tab_scales, offs, offs2, offs3, offs4, w1, w2_words, w2_scales,
              gain, wgs, page0, w3, w4_words, w4_scales, bias):
    v = unpack_weight(tab_words, tab_scales, "e4m3")[:, unstriped(offs)]
    w2 = unpack_weight(w2_words, w2_scales, "e2m1")
    w4 = unpack_weight(w4_words, w4_scales, "e4m3")
    level = np.sqrt(np.abs(mxq(f64(w1), 0, "e4m3").T @ v))
    h = level * (w2.T @ v) * f64(gain)[:, None]
    before = f64(page0)
    page = before.copy()
    page[:, unstriped(offs2)] = np.tile(f64(wgs), (H // 128, 1)) * h
    x = page[:, unstriped(offs3)] - before[:, unstriped(offs4)]
    change = w4.T @ mxq(x, 0, "e4m3")
    spectral = mxq(f64(w3), 0, "e4m3").T @ v
    return np.maximum(change, spectral) + f64(bias)[:, None]

@@ -1,0 +1,288 @@
+from contextlib import ExitStack
+
+import concourse.mybir as mybir
+
+K, T, S, H, T2, N = 1024, 2048, 1024, 512, 2048, 384
+FLOPS = 2 * K * H * S * 2 + 2 * K * N * S + 2 * H * N * S
+
+F32 = mybir.dt.float32
+BF16 = mybir.dt.bfloat16
+I32 = mybir.dt.int32
+U32 = mybir.dt.uint32
+U16 = mybir.dt.uint16
+U8 = mybir.dt.uint8
+FP8X4 = mybir.dt.float8_e4m3fn_x4
+FP4X4 = mybir.dt.float4_e2m1fn_x4
+ALU = mybir.AluOpType
+ACT = mybir.ActivationFunctionType
+
+P = 128
+PACK = 4
+K_PASS = P * PACK
+PASSES = K // K_PASS
+QUADS = 4
+QUAD = 32
+BANK = 512
+N_TILES = N // P
+CHUNKS = (256, 256, 256, 256)
+
+
+def tile_list_tailings_beach_drying_kernel(
+    tc, tab_words, tab_scales, offs, offs2, offs3, offs4, w1, w2_words, w2_scales, gain, wgs, page0, w3, w4_words, w4_scales, bias, out
+):
+    nc = tc.nc
+    with ExitStack() as ctx:
+        keep = ctx.enter_context(tc.tile_pool(name="keep", bufs=1))
+        work = ctx.enter_context(tc.tile_pool(name="work", bufs=2))
+        reuse = ctx.enter_context(tc.tile_pool(name="reuse", bufs=1))
+        psum = ctx.enter_context(tc.psum_pool(name="psum", bufs=2))
+
+        def held(shape, dtype, name):
+            return keep.tile(shape, dtype, name=name, align_bytes=64)
+
+        pixel_list = held([P, S // 16], U16, "pixel_list")
+        put_list = held([P, S // 16], U16, "put_list")
+        after_list = held([P, S // 16], U16, "after_list")
+        before_list = held([P, S // 16], U16, "before_list")
+
+        tab_sc = held([P, T], U8, "tab_sc")
+        tab_w = [reuse.tile([P, T], I32, name=f"tab_w{a}", align_bytes=64, offset=4 * T * a) for a in range(PASSES)]
+        v_w = [held([P, S], U32, f"v_w{a}") for a in range(PASSES)]
+        v_sc = reuse.tile([P, S], U8, name="v_sc", align_bytes=64, offset=0)
+        v_sc1 = held([P, S], U8, "v_sc1")
+        w2_raw = held([P, PASSES, 2 * H], U8, "w2_raw")
+        w2_sc_raw = held([P, PASSES, H], U8, "w2_sc_raw")
+        w2_w = reuse.tile([P, PASSES, 2 * H], U8, name="w2_w", align_bytes=64, offset=4 * T)
+        w2_sc = reuse.tile([P, PASSES, H], U8, name="w2_sc", align_bytes=64, offset=4 * T + 4 * H)
+        w4_w = held([P, N], I32, "w4_w")
+        w4_sc = held([P, N], U8, "w4_sc")
+        w1_raw = [held([P, PACK, H], F32, f"w1_raw{a}") for a in range(PASSES)]
+        w3_raw = [held([P, PACK, N], F32, f"w3_raw{a}") for a in range(PASSES)]
+        page = [held([P, T2], F32, f"page{t}") for t in range(PACK)]
+        before = {}
+        wgs_first = held([P, S], F32, "wgs_first")
+        wgs_rest = held([P, PACK - 1, S], F32, "wgs_rest")
+        gain_sb = held([P, PACK], F32, "gain_sb")
+        bias_sb = held([P, N_TILES], F32, "bias_sb")
+
+        nc.vector.memset(tab_sc[:].bitcast(I32), 0)
+        nc.vector.memset(w2_sc_raw[:].rearrange("p a n -> p (a n)").bitcast(I32), 0)
+        nc.vector.memset(v_sc1[:].bitcast(I32), 0)
+        nc.vector.memset(w4_sc[:].bitcast(I32), 0)
+
+        page_rows = page0.rearrange("(p t) c -> t p c", t=PACK)
+        wgs_rows = wgs.rearrange("(q t) j -> q t j", t=PACK)
+
+        def load_table(a):
+            nc.sync.dma_start(out=tab_w[a][:], in_=tab_words[a].rearrange("p n i -> p (n i)").bitcast(I32))
+
+        def load_rows(dst, src, a):
+            nc.sync.dma_start(out=dst[a][:], in_=src[a * K_PASS : (a + 1) * K_PASS, :].rearrange("(p j) c -> p j c", j=PACK))
+
+        nc.sync.dma_start(pixel_list[:], offs)
+        for q in range(QUADS):
+            nc.scalar.dma_start(
+                out=tab_sc[QUAD * q : QUAD * q + 4 * PASSES, :].bitcast(I32),
+                in_=tab_scales[:, 4 * q : 4 * q + 4, :].bitcast(I32),
+            )
+        load_table(0)
+        load_table(1)
+        nc.sync.dma_start(before_list[:], offs4)
+        nc.sync.dma_start(out=w2_raw[:].bitcast(I32), in_=w2_words.rearrange("a p n -> p a n").bitcast(I32))
+        for q in range(QUADS):
+            nc.sync.dma_start(
+                out=w2_sc_raw[QUAD * q : QUAD * q + 4, :, :].bitcast(I32),
+                in_=w2_scales[:, 4 * q : 4 * q + 4, :].rearrange("a r n -> r a n").bitcast(I32),
+            )
+        load_rows(w1_raw, w1, 0)
+        nc.sync.dma_start(out=page[0][:], in_=page_rows[0])
+        load_rows(w1_raw, w1, 1)
+        nc.sync.dma_start(out=page[1][:], in_=page_rows[1])
+        nc.sync.dma_start(out=gain_sb[:], in_=gain.rearrange("(p t) -> p t", t=PACK))
+        nc.sync.dma_start(put_list[:], offs2)
+        for q in range(QUADS):
+            nc.sync.dma_start(out=wgs_first[QUAD * q : QUAD * (q + 1), :], in_=wgs_rows[:, 0, :])
+        nc.sync.dma_start(after_list[:], offs3)
+        with nc.allow_non_contiguous_dma(reason="one bias value a partition"):
+            nc.sync.dma_start(out=bias_sb[:], in_=bias.rearrange("(c p) -> p c", p=P))
+        load_rows(w3_raw, w3, 0)
+        load_rows(w3_raw, w3, 1)
+        for q in range(QUADS):
+            nc.sync.dma_start(out=wgs_rest[QUAD * q : QUAD * (q + 1), :, :], in_=wgs_rows[:, 1:PACK, :])
+        nc.sync.dma_start(out=page[2][:], in_=page_rows[2])
+        nc.sync.dma_start(out=page[3][:], in_=page_rows[3])
+        nc.sync.dma_start(out=w4_w[:], in_=w4_words[0].rearrange("p n i -> p (n i)").bitcast(I32))
+        for q in range(QUADS):
+            nc.sync.dma_start(
+                out=w4_sc[QUAD * q : QUAD * q + 4, :].bitcast(I32),
+                in_=w4_scales[0, 4 * q : 4 * q + 4, :].bitcast(I32),
+            )
+
+        nc.vector.tensor_copy(v_w[0][:], tab_w[0][:].bitcast(U32).indirect(pixel_list[:]))
+        nc.vector.tensor_copy(v_sc[:], tab_sc[:].indirect(pixel_list[:]))
+        for q in range(QUADS):
+            nc.gpsimd.dma_start(
+                out=v_sc1[QUAD * q : QUAD * q + 4, :].bitcast(I32),
+                in_=v_sc[QUAD * q + 4 : QUAD * q + 8, :].bitcast(I32),
+            )
+        nc.vector.tensor_copy(v_w[1][:], tab_w[1][:].bitcast(U32).indirect(pixel_list[:]))
+
+        nc.vector.tensor_copy(
+            out=w2_w[:].bitcast(U16).rearrange("p a (t m) -> p a t m", t=PACK),
+            in_=w2_raw[:].bitcast(U16).rearrange("p a (m t) -> p a t m", t=PACK),
+        )
+        nc.vector.tensor_copy(
+            out=w2_sc[:].rearrange("p a (t m) -> p a t m", t=PACK),
+            in_=w2_sc_raw[:].rearrange("p a (m t) -> p a t m", t=PACK),
+        )
+
+        def shared(shape, dtype, name, tag):
+            return keep.tile(shape, dtype, name=name, tag=tag, align_bytes=64)
+
+        def fetch_before(t):
+            before[t] = shared([P, S], F32, f"before{t}", ("before0", "w1_grouped1", "h0", "h1")[t])
+            nc.vector.tensor_copy(before[t][:], page[t][:].indirect(before_list[:]))
+
+        w1_w = [held([P, H], U32, f"w1_w{a}") for a in range(PASSES)]
+        w1_sc = [held([P, H], U8, f"w1_sc{a}") for a in range(PASSES)]
+        w3_w = [held([P, N], U32, f"w3_w{a}") for a in range(PASSES)]
+        w3_sc = [held([P, N], U8, f"w3_sc{a}") for a in range(PASSES)]
+
+        def quantise_w1(a):
+            grouped = shared([P, PACK * H], BF16, f"w1_grouped{a}", f"w1_grouped{a}")
+            nc.scalar.copy(
+                out=grouped[:].rearrange("p (t m j) -> p m j t", t=PACK, j=PACK),
+                in_=w1_raw[a][:].rearrange("p j (m t) -> p m j t", t=PACK),
+            )
+            nc.vector.quantize_mx(out=w1_w[a][:].bitcast(FP8X4), scales=w1_sc[a][:], in_=grouped[:])
+
+        def quantise_w3(a):
+            grouped = shared([P, PACK * N], BF16, f"w3_grouped{a}", f"level{a}")
+            nc.scalar.copy(
+                out=grouped[:].rearrange("p (c i j) -> p c j i", i=4, j=PACK),
+                in_=w3_raw[a][:].rearrange("p j (c i) -> p c j i", i=4),
+            )
+            nc.vector.quantize_mx(out=w3_w[a][:].bitcast(FP8X4), scales=w3_sc[a][:], in_=grouped[:])
+
+        fetch_before(0)
+        quantise_w1(0)
+        quantise_w1(1)
+        fetch_before(1)
+
+        def table_product(acc, words, scales, cols, packed_planes):
+            for a in range(PASSES):
+                if a == 0:
+                    plane = v_sc[:, cols]
+                elif packed_planes:
+                    plane = v_sc[4:P, cols]
+                else:
+                    plane = v_sc1[:, cols]
+                nc.tensor.matmul_mx(
+                    out=acc,
+                    lhsT=words(a),
+                    lhsT_scale=scales(a),
+                    rhs=v_w[a][:, cols].bitcast(FP8X4),
+                    rhs_scale=plane,
+                    start=(a == 0),
+                    stop=(a == PASSES - 1),
+                )
+
+        def new_columns(t):
+            h = shared([P, S], F32, f"h{t}", f"h{t}")
+            level = shared([P, S], F32, f"level{t}", f"level{t}")
+            rows = slice(P * t, P * (t + 1))
+            for j0 in range(0, S, BANK):
+                cols = slice(j0, j0 + BANK)
+                acc1 = psum.tile([P, BANK], F32, name="acc1", tag="acc1")
+                acc2 = psum.tile([P, BANK], F32, name="acc2", tag="acc2", bufs=3)
+                table_product(acc1[:], lambda a: w1_w[a][:, rows].bitcast(FP8X4), lambda a: w1_sc[a][:, rows], cols, True)
+                table_product(
+                    acc2[:], lambda a: w2_w[:, a, 2 * P * t : 2 * P * (t + 1)].bitcast(FP4X4), lambda a: w2_sc[:, a, rows], cols, False
+                )
+                size = work.tile([P, BANK], F32, name="size", tag="size")
+                nc.scalar.activation(out=size[:], in_=acc1[:], func=ACT.Abs)
+                nc.scalar.activation(out=level[:, cols], in_=size[:], func=ACT.Sqrt)
+                nc.vector.scalar_tensor_tensor(
+                    out=h[:, cols], in0=acc2[:], scalar=gain_sb[:, t : t + 1], in1=level[:, cols], op0=ALU.mult, op1=ALU.mult
+                )
+            return h
+
+        def put(t, h):
+            weights = wgs_first[:] if t == 0 else wgs_rest[:, t - 1, :]
+            nc.vector.tensor_tensor(page[t][:].indirect(put_list[:]), h[:], weights, ALU.mult)
+
+        x = held([P, PACK, S], F32, "x")
+
+        def fetch_after(t, j0, width):
+            nc.vector.tensor_tensor(
+                x[:, t, j0 : j0 + width],
+                page[t][:].indirect(after_list[:, j0 // 16 : (j0 + width) // 16]),
+                before[t][:, j0 : j0 + width],
+                ALU.subtract,
+            )
+
+        spectral = [held([P, S], F32, f"spectral{c}") for c in range(N_TILES)]
+
+        def spectral_scores():
+            for c in range(N_TILES):
+                rows = slice(P * c, P * (c + 1))
+                for j0 in range(0, S, BANK):
+                    cols = slice(j0, j0 + BANK)
+                    acc3 = psum.tile([P, BANK], F32, name="acc3", tag="acc3", bufs=3)
+                    table_product(acc3[:], lambda a: w3_w[a][:, rows].bitcast(FP8X4), lambda a: w3_sc[a][:, rows], cols, True)
+                    nc.scalar.activation(out=spectral[c][:, cols], in_=acc3[:], func=ACT.Identity, bias=bias_sb[:, c : c + 1])
+
+        for t in range(PACK):
+            h = new_columns(t)
+            put(t, h)
+            if t + 2 < PACK:
+                fetch_before(t + 2)
+            if t < PASSES:
+                quantise_w3(t)
+            if t == PASSES - 1:
+                spectral_scores()
+            if t + 1 < PACK:
+                fetch_after(t, 0, S)
+
+        out_rows = out.rearrange("(c p) j -> p c j", p=P)
+        starts = [sum(CHUNKS[:i]) for i in range(len(CHUNKS))]
+        x_w, x_sc = {}, {}
+
+        def quantise_x(i):
+            j0, width = starts[i], CHUNKS[i]
+            fetch_after(PACK - 1, j0, width)
+            grouped = shared([P, PACK * width], BF16, f"x_grouped{i}", f"x_grouped{i}")
+            nc.scalar.copy(
+                out=grouped[:].rearrange("p (c i t) -> p c t i", i=4, t=PACK),
+                in_=x[:, :, j0 : j0 + width].rearrange("p t (c i) -> p c t i", i=4),
+            )
+            x_w[i] = held([P, width], U32, f"x_w{i}")
+            x_sc[i] = held([P, width], U8, f"x_sc{i}")
+            nc.vector.quantize_mx(out=x_w[i][:].bitcast(FP8X4), scales=x_sc[i][:], in_=grouped[:])
+
+        def score(i):
+            width = CHUNKS[i]
+            cols = slice(starts[i], starts[i] + width)
+            result = shared([P, N_TILES, width], F32, f"result{i}", f"x_grouped{i + 1}")
+            for c in range(N_TILES):
+                rows = slice(P * c, P * (c + 1))
+                acc4 = psum.tile([P, width], F32, name="acc4", tag=("acc3", "acc2")[i % 2], bufs=3)
+                nc.tensor.matmul_mx(
+                    out=acc4[:],
+                    lhsT=w4_w[:, rows].bitcast(FP8X4),
+                    lhsT_scale=w4_sc[:, rows],
+                    rhs=x_w[i][:].bitcast(FP8X4),
+                    rhs_scale=x_sc[i][:],
+                    start=True,
+                    stop=True,
+                )
+                nc.vector.scalar_tensor_tensor(
+                    out=result[:, c, :], in0=acc4[:], scalar=bias_sb[:, c : c + 1], in1=spectral[c][:, cols], op0=ALU.add, op1=ALU.max
+                )
+            nc.sync.dma_start(out=out_rows[:, :, cols], in_=result[:])
+
+        quantise_x(0)
+        for i in range(len(CHUNKS)):
+            if i + 1 < len(CHUNKS):
+                quantise_x(i + 1)
+            score(i)

@@ -52,7 +52,7 @@ def tile_list_tailings_beach_drying_kernel(
         v_sc1 = held([P, S], U8, "v_sc1")
         w2_raw = held([P, PASSES, 2 * H], U8, "w2_raw")
         w2_sc_raw = held([P, PASSES, H], U8, "w2_sc_raw")
-        w2_w = reuse.tile([P, PASSES, 2 * H], U8, name="w2_w", align_bytes=64, offset=4 * T)
+        w2_w = held([P, PASSES, 2 * H], U8, "w2_w")
         w2_sc = reuse.tile([P, PASSES, H], U8, name="w2_sc", align_bytes=64, offset=4 * T + 4 * H)
         w4_w = held([P, N], I32, "w4_w")
         w4_sc = held([P, N], U8, "w4_sc")
@@ -97,20 +97,28 @@ def tile_list_tailings_beach_drying_kernel(
         load_rows(w1_raw, w1, 0)
         nc.sync.dma_start(out=page[0][:], in_=page_rows[0])
         load_rows(w1_raw, w1, 1)
+
+        nc.vector.tensor_copy(v_w[0][:], tab_w[0][:].bitcast(U32).indirect(pixel_list[:]))
+        nc.vector.tensor_copy(v_sc[:], tab_sc[:].indirect(pixel_list[:]))
+        for q in range(QUADS):
+            nc.sync.dma_start(
+                out=v_sc1[QUAD * q : QUAD * q + 4, :].bitcast(I32),
+                in_=v_sc[QUAD * q + 4 : QUAD * q + 8, :].bitcast(I32),
+            )
         nc.sync.dma_start(out=page[1][:], in_=page_rows[1])
         nc.sync.dma_start(out=gain_sb[:], in_=gain.rearrange("(p t) -> p t", t=PACK))
         nc.sync.dma_start(put_list[:], offs2)
-        for q in range(QUADS):
+        for q in (0, 2, 1, 3):
             nc.sync.dma_start(out=wgs_first[QUAD * q : QUAD * (q + 1), :], in_=wgs_rows[:, 0, :])
         nc.sync.dma_start(after_list[:], offs3)
-        with nc.allow_non_contiguous_dma(reason="one bias value a partition"):
-            nc.sync.dma_start(out=bias_sb[:], in_=bias.rearrange("(c p) -> p c", p=P))
+        nc.sync.dma_start(out=page[2][:], in_=page_rows[2])
+        for q in (0, 2, 1, 3):
+            nc.sync.dma_start(out=wgs_rest[QUAD * q : QUAD * (q + 1), :, :], in_=wgs_rows[:, 1:PACK, :])
         load_rows(w3_raw, w3, 0)
         load_rows(w3_raw, w3, 1)
-        for q in range(QUADS):
-            nc.sync.dma_start(out=wgs_rest[QUAD * q : QUAD * (q + 1), :, :], in_=wgs_rows[:, 1:PACK, :])
-        nc.sync.dma_start(out=page[2][:], in_=page_rows[2])
         nc.sync.dma_start(out=page[3][:], in_=page_rows[3])
+        with nc.allow_non_contiguous_dma(reason="one bias value a partition"):
+            nc.sync.dma_start(out=bias_sb[:], in_=bias.rearrange("(c p) -> p c", p=P))
         nc.sync.dma_start(out=w4_w[:], in_=w4_words[0].rearrange("p n i -> p (n i)").bitcast(I32))
         for q in range(QUADS):
             nc.sync.dma_start(
@@ -118,16 +126,9 @@ def tile_list_tailings_beach_drying_kernel(
                 in_=w4_scales[0, 4 * q : 4 * q + 4, :].bitcast(I32),
             )
 
-        nc.vector.tensor_copy(v_w[0][:], tab_w[0][:].bitcast(U32).indirect(pixel_list[:]))
-        nc.vector.tensor_copy(v_sc[:], tab_sc[:].indirect(pixel_list[:]))
-        for q in range(QUADS):
-            nc.gpsimd.dma_start(
-                out=v_sc1[QUAD * q : QUAD * q + 4, :].bitcast(I32),
-                in_=v_sc[QUAD * q + 4 : QUAD * q + 8, :].bitcast(I32),
-            )
         nc.vector.tensor_copy(v_w[1][:], tab_w[1][:].bitcast(U32).indirect(pixel_list[:]))
 
-        nc.vector.tensor_copy(
+        nc.scalar.copy(
             out=w2_w[:].bitcast(U16).rearrange("p a (t m) -> p a t m", t=PACK),
             in_=w2_raw[:].bitcast(U16).rearrange("p a (m t) -> p a t m", t=PACK),
         )
@@ -140,7 +141,7 @@ def tile_list_tailings_beach_drying_kernel(
             return keep.tile(shape, dtype, name=name, tag=tag, align_bytes=64)
 
         def fetch_before(t):
-            before[t] = shared([P, S], F32, f"before{t}", ("before0", "w1_grouped1", "h0", "h1")[t])
+            before[t] = shared([P, S], F32, f"before{t}", ("before0", "w1_grouped1_0", "h0", "h1")[t])
             nc.vector.tensor_copy(before[t][:], page[t][:].indirect(before_list[:]))
 
         w1_w = [held([P, H], U32, f"w1_w{a}") for a in range(PASSES)]
@@ -156,17 +157,27 @@ def tile_list_tailings_beach_drying_kernel(
             )
             nc.vector.quantize_mx(out=w1_w[a][:].bitcast(FP8X4), scales=w1_sc[a][:], in_=grouped[:])
 
-        def quantise_w3(a):
-            grouped = shared([P, PACK * N], BF16, f"w3_grouped{a}", f"level{a}")
-            nc.scalar.copy(
-                out=grouped[:].rearrange("p (c i j) -> p c j i", i=4, j=PACK),
-                in_=w3_raw[a][:].rearrange("p j (c i) -> p c j i", i=4),
-            )
-            nc.vector.quantize_mx(out=w3_w[a][:].bitcast(FP8X4), scales=w3_sc[a][:], in_=grouped[:])
+        def quantise_w1_split(a):
+            for t0, t1 in ((0, 1), (1, PACK)):
+                part = shared([P, H * (t1 - t0)], BF16, f"w1_grouped{a}_{t0}", f"w1_grouped{a}_{t0}")[:]
+                nc.scalar.copy(
+                    out=part.rearrange("p (t m j) -> p m j t", t=t1 - t0, j=PACK),
+                    in_=w1_raw[a][:].rearrange("p j (m t) -> p m j t", t=PACK)[:, :, :, t0:t1],
+                )
+                nc.vector.quantize_mx(out=w1_w[a][:, P * t0 : P * t1].bitcast(FP8X4), scales=w1_sc[a][:, P * t0 : P * t1], in_=part)
+
+        def quantise_w3():
+            grouped = shared([P, PASSES, PACK * N], BF16, "w3_grouped", "level1")
+            for a in range(PASSES):
+                nc.scalar.copy(
+                    out=grouped[:, a, :].rearrange("p (c i j) -> p c j i", i=4, j=PACK),
+                    in_=w3_raw[a][:].rearrange("p j (c i) -> p c j i", i=4),
+                )
+                nc.vector.quantize_mx(out=w3_w[a][:].bitcast(FP8X4), scales=w3_sc[a][:], in_=grouped[:, a, :])
 
         fetch_before(0)
         quantise_w1(0)
-        quantise_w1(1)
+        quantise_w1_split(1)
         fetch_before(1)
 
         def table_product(acc, words, scales, cols, packed_planes):
@@ -188,7 +199,7 @@ def tile_list_tailings_beach_drying_kernel(
                 )
 
         def new_columns(t):
-            h = shared([P, S], F32, f"h{t}", f"h{t}")
+            h = shared([P, S], F32, f"h{t}", ("h0", "h1", "h2", "level1")[t])
             level = shared([P, S], F32, f"level{t}", f"level{t}")
             rows = slice(P * t, P * (t + 1))
             for j0 in range(0, S, BANK):
@@ -237,9 +248,8 @@ def tile_list_tailings_beach_drying_kernel(
             put(t, h)
             if t + 2 < PACK:
                 fetch_before(t + 2)
-            if t < PASSES:
-                quantise_w3(t)
-            if t == PASSES - 1:
+            if t == 1:
+                quantise_w3()
                 spectral_scores()
             if t + 1 < PACK:
                 fetch_after(t, 0, S)

@@ -65,6 +65,11 @@ def tile_list_tailings_beach_drying_kernel(
         gain_sb = held([P, PACK], F32, "gain_sb")
         bias_sb = held([P, N_TILES], F32, "bias_sb")
 
+        one = held([P, 1], F32, "one")
+        root_of_one = held([P, 1], F32, "root_of_one")
+        nc.gpsimd.memset(one[:], 1.0)
+        nc.scalar.activation(out=root_of_one[:], in_=one[:], func=ACT.Sqrt)
+
         nc.vector.memset(tab_sc[:].bitcast(I32), 0)
         nc.vector.memset(w2_sc_raw[:].rearrange("p a n -> p (a n)").bitcast(I32), 0)
         nc.vector.memset(v_sc1[:].bitcast(I32), 0)

from contextlib import ExitStack

import concourse.mybir as mybir

K, T, S, H, T2, N = 1024, 2048, 1024, 512, 2048, 384
FLOPS = 2 * K * H * S * 2 + 2 * K * N * S + 2 * H * N * S

F32 = mybir.dt.float32
BF16 = mybir.dt.bfloat16
I32 = mybir.dt.int32
U32 = mybir.dt.uint32
U16 = mybir.dt.uint16
U8 = mybir.dt.uint8
FP8X4 = mybir.dt.float8_e4m3fn_x4
FP4X4 = mybir.dt.float4_e2m1fn_x4
ALU = mybir.AluOpType
ACT = mybir.ActivationFunctionType

P = 128
PACK = 4
K_PASS = P * PACK
PASSES = K // K_PASS
QUADS = 4
QUAD = 32
BANK = 512
N_TILES = N // P
CHUNKS = (256, 256, 256, 256)


def tile_list_tailings_beach_drying_kernel(
    tc, tab_words, tab_scales, offs, offs2, offs3, offs4, w1, w2_words, w2_scales, gain, wgs, page0, w3, w4_words, w4_scales, bias, out
):
    nc = tc.nc
    with ExitStack() as ctx:
        keep = ctx.enter_context(tc.tile_pool(name="keep", bufs=1))
        work = ctx.enter_context(tc.tile_pool(name="work", bufs=2))
        reuse = ctx.enter_context(tc.tile_pool(name="reuse", bufs=1))
        psum = ctx.enter_context(tc.psum_pool(name="psum", bufs=2))

        def held(shape, dtype, name):
            return keep.tile(shape, dtype, name=name, align_bytes=64)

        pixel_list = held([P, S // 16], U16, "pixel_list")
        put_list = held([P, S // 16], U16, "put_list")
        after_list = held([P, S // 16], U16, "after_list")
        before_list = held([P, S // 16], U16, "before_list")

        tab_sc = held([P, T], U8, "tab_sc")
        tab_w = [reuse.tile([P, T], I32, name=f"tab_w{a}", align_bytes=64, offset=4 * T * a) for a in range(PASSES)]
        v_w = [held([P, S], U32, f"v_w{a}") for a in range(PASSES)]
        v_sc = reuse.tile([P, S], U8, name="v_sc", align_bytes=64, offset=0)
        v_sc1 = held([P, S], U8, "v_sc1")
        w2_raw = held([P, PASSES, 2 * H], U8, "w2_raw")
        w2_sc_raw = held([P, PASSES, H], U8, "w2_sc_raw")
        w2_w = held([P, PASSES, 2 * H], U8, "w2_w")
        w2_sc = reuse.tile([P, PASSES, H], U8, name="w2_sc", align_bytes=64, offset=4 * T + 4 * H)
        w4_w = held([P, N], I32, "w4_w")
        w4_sc = held([P, N], U8, "w4_sc")
        w1_raw = [held([P, PACK, H], F32, f"w1_raw{a}") for a in range(PASSES)]
        w3_raw = [held([P, PACK, N], F32, f"w3_raw{a}") for a in range(PASSES)]
        page = [held([P, T2], F32, f"page{t}") for t in range(PACK)]
        before = {}
        wgs_first = held([P, S], F32, "wgs_first")
        wgs_rest = held([P, PACK - 1, S], F32, "wgs_rest")
        gain_sb = held([P, PACK], F32, "gain_sb")
        bias_sb = held([P, N_TILES], F32, "bias_sb")

        one = held([P, 1], F32, "one")
        root_of_one = held([P, 1], F32, "root_of_one")
        nc.gpsimd.memset(one[:], 1.0)
        nc.scalar.activation(out=root_of_one[:], in_=one[:], func=ACT.Sqrt)

        nc.vector.memset(tab_sc[:].bitcast(I32), 0)
        nc.vector.memset(w2_sc_raw[:].rearrange("p a n -> p (a n)").bitcast(I32), 0)
        nc.vector.memset(v_sc1[:].bitcast(I32), 0)
        nc.vector.memset(w4_sc[:].bitcast(I32), 0)

        page_rows = page0.rearrange("(p t) c -> t p c", t=PACK)
        wgs_rows = wgs.rearrange("(q t) j -> q t j", t=PACK)

        def load_table(a):
            nc.sync.dma_start(out=tab_w[a][:], in_=tab_words[a].rearrange("p n i -> p (n i)").bitcast(I32))

        def load_rows(dst, src, a):
            nc.sync.dma_start(out=dst[a][:], in_=src[a * K_PASS : (a + 1) * K_PASS, :].rearrange("(p j) c -> p j c", j=PACK))

        nc.sync.dma_start(pixel_list[:], offs)
        for q in range(QUADS):
            nc.scalar.dma_start(
                out=tab_sc[QUAD * q : QUAD * q + 4 * PASSES, :].bitcast(I32),
                in_=tab_scales[:, 4 * q : 4 * q + 4, :].bitcast(I32),
            )
        load_table(0)
        load_table(1)
        nc.sync.dma_start(before_list[:], offs4)
        nc.sync.dma_start(out=w2_raw[:].bitcast(I32), in_=w2_words.rearrange("a p n -> p a n").bitcast(I32))
        for q in range(QUADS):
            nc.sync.dma_start(
                out=w2_sc_raw[QUAD * q : QUAD * q + 4, :, :].bitcast(I32),
                in_=w2_scales[:, 4 * q : 4 * q + 4, :].rearrange("a r n -> r a n").bitcast(I32),
            )
        load_rows(w1_raw, w1, 0)
        nc.sync.dma_start(out=page[0][:], in_=page_rows[0])
        load_rows(w1_raw, w1, 1)

        nc.vector.tensor_copy(v_w[0][:], tab_w[0][:].bitcast(U32).indirect(pixel_list[:]))
        nc.vector.tensor_copy(v_sc[:], tab_sc[:].indirect(pixel_list[:]))
        for q in range(QUADS):
            nc.sync.dma_start(
                out=v_sc1[QUAD * q : QUAD * q + 4, :].bitcast(I32),
                in_=v_sc[QUAD * q + 4 : QUAD * q + 8, :].bitcast(I32),
            )
        nc.sync.dma_start(out=page[1][:], in_=page_rows[1])
        nc.sync.dma_start(out=gain_sb[:], in_=gain.rearrange("(p t) -> p t", t=PACK))
        nc.sync.dma_start(put_list[:], offs2)
        for q in (0, 2, 1, 3):
            nc.sync.dma_start(out=wgs_first[QUAD * q : QUAD * (q + 1), :], in_=wgs_rows[:, 0, :])
        nc.sync.dma_start(after_list[:], offs3)
        nc.sync.dma_start(out=page[2][:], in_=page_rows[2])
        for q in (0, 2, 1, 3):
            nc.sync.dma_start(out=wgs_rest[QUAD * q : QUAD * (q + 1), :, :], in_=wgs_rows[:, 1:PACK, :])
        load_rows(w3_raw, w3, 0)
        load_rows(w3_raw, w3, 1)
        nc.sync.dma_start(out=page[3][:], in_=page_rows[3])
        with nc.allow_non_contiguous_dma(reason="one bias value a partition"):
            nc.sync.dma_start(out=bias_sb[:], in_=bias.rearrange("(c p) -> p c", p=P))
        nc.sync.dma_start(out=w4_w[:], in_=w4_words[0].rearrange("p n i -> p (n i)").bitcast(I32))
        for q in range(QUADS):
            nc.sync.dma_start(
                out=w4_sc[QUAD * q : QUAD * q + 4, :].bitcast(I32),
                in_=w4_scales[0, 4 * q : 4 * q + 4, :].bitcast(I32),
            )

        nc.vector.tensor_copy(v_w[1][:], tab_w[1][:].bitcast(U32).indirect(pixel_list[:]))

        nc.scalar.copy(
            out=w2_w[:].bitcast(U16).rearrange("p a (t m) -> p a t m", t=PACK),
            in_=w2_raw[:].bitcast(U16).rearrange("p a (m t) -> p a t m", t=PACK),
        )
        nc.vector.tensor_copy(
            out=w2_sc[:].rearrange("p a (t m) -> p a t m", t=PACK),
            in_=w2_sc_raw[:].rearrange("p a (m t) -> p a t m", t=PACK),
        )

        def shared(shape, dtype, name, tag):
            return keep.tile(shape, dtype, name=name, tag=tag, align_bytes=64)

        def fetch_before(t):
            before[t] = shared([P, S], F32, f"before{t}", ("before0", "w1_grouped1_0", "h0", "h1")[t])
            nc.vector.tensor_copy(before[t][:], page[t][:].indirect(before_list[:]))

        w1_w = [held([P, H], U32, f"w1_w{a}") for a in range(PASSES)]
        w1_sc = [held([P, H], U8, f"w1_sc{a}") for a in range(PASSES)]
        w3_w = [held([P, N], U32, f"w3_w{a}") for a in range(PASSES)]
        w3_sc = [held([P, N], U8, f"w3_sc{a}") for a in range(PASSES)]

        def quantise_w1(a):
            grouped = shared([P, PACK * H], BF16, f"w1_grouped{a}", f"w1_grouped{a}")
            nc.scalar.copy(
                out=grouped[:].rearrange("p (t m j) -> p m j t", t=PACK, j=PACK),
                in_=w1_raw[a][:].rearrange("p j (m t) -> p m j t", t=PACK),
            )
            nc.vector.quantize_mx(out=w1_w[a][:].bitcast(FP8X4), scales=w1_sc[a][:], in_=grouped[:])

        def quantise_w1_split(a):
            for t0, t1 in ((0, 1), (1, PACK)):
                part = shared([P, H * (t1 - t0)], BF16, f"w1_grouped{a}_{t0}", f"w1_grouped{a}_{t0}")[:]
                nc.scalar.copy(
                    out=part.rearrange("p (t m j) -> p m j t", t=t1 - t0, j=PACK),
                    in_=w1_raw[a][:].rearrange("p j (m t) -> p m j t", t=PACK)[:, :, :, t0:t1],
                )
                nc.vector.quantize_mx(out=w1_w[a][:, P * t0 : P * t1].bitcast(FP8X4), scales=w1_sc[a][:, P * t0 : P * t1], in_=part)

        def quantise_w3():
            grouped = shared([P, PASSES, PACK * N], BF16, "w3_grouped", "level1")
            for a in range(PASSES):
                nc.scalar.copy(
                    out=grouped[:, a, :].rearrange("p (c i j) -> p c j i", i=4, j=PACK),
                    in_=w3_raw[a][:].rearrange("p j (c i) -> p c j i", i=4),
                )
                nc.vector.quantize_mx(out=w3_w[a][:].bitcast(FP8X4), scales=w3_sc[a][:], in_=grouped[:, a, :])

        fetch_before(0)
        quantise_w1(0)
        quantise_w1_split(1)
        fetch_before(1)

        def table_product(acc, words, scales, cols, packed_planes):
            for a in range(PASSES):
                if a == 0:
                    plane = v_sc[:, cols]
                elif packed_planes:
                    plane = v_sc[4:P, cols]
                else:
                    plane = v_sc1[:, cols]
                nc.tensor.matmul_mx(
                    out=acc,
                    lhsT=words(a),
                    lhsT_scale=scales(a),
                    rhs=v_w[a][:, cols].bitcast(FP8X4),
                    rhs_scale=plane,
                    start=(a == 0),
                    stop=(a == PASSES - 1),
                )

        def new_columns(t):
            h = shared([P, S], F32, f"h{t}", ("h0", "h1", "h2", "level1")[t])
            level = shared([P, S], F32, f"level{t}", f"level{t}")
            rows = slice(P * t, P * (t + 1))
            for j0 in range(0, S, BANK):
                cols = slice(j0, j0 + BANK)
                acc1 = psum.tile([P, BANK], F32, name="acc1", tag="acc1")
                acc2 = psum.tile([P, BANK], F32, name="acc2", tag="acc2", bufs=3)
                table_product(acc1[:], lambda a: w1_w[a][:, rows].bitcast(FP8X4), lambda a: w1_sc[a][:, rows], cols, True)
                table_product(
                    acc2[:], lambda a: w2_w[:, a, 2 * P * t : 2 * P * (t + 1)].bitcast(FP4X4), lambda a: w2_sc[:, a, rows], cols, False
                )
                size = work.tile([P, BANK], F32, name="size", tag="size")
                nc.scalar.activation(out=size[:], in_=acc1[:], func=ACT.Abs)
                nc.scalar.activation(out=level[:, cols], in_=size[:], func=ACT.Sqrt)
                nc.vector.scalar_tensor_tensor(
                    out=h[:, cols], in0=acc2[:], scalar=gain_sb[:, t : t + 1], in1=level[:, cols], op0=ALU.mult, op1=ALU.mult
                )
            return h

        def put(t, h):
            weights = wgs_first[:] if t == 0 else wgs_rest[:, t - 1, :]
            nc.vector.tensor_tensor(page[t][:].indirect(put_list[:]), h[:], weights, ALU.mult)

        x = held([P, PACK, S], F32, "x")

        def fetch_after(t, j0, width):
            nc.vector.tensor_tensor(
                x[:, t, j0 : j0 + width],
                page[t][:].indirect(after_list[:, j0 // 16 : (j0 + width) // 16]),
                before[t][:, j0 : j0 + width],
                ALU.subtract,
            )

        spectral = [held([P, S], F32, f"spectral{c}") for c in range(N_TILES)]

        def spectral_scores():
            for c in range(N_TILES):
                rows = slice(P * c, P * (c + 1))
                for j0 in range(0, S, BANK):
                    cols = slice(j0, j0 + BANK)
                    acc3 = psum.tile([P, BANK], F32, name="acc3", tag="acc3", bufs=3)
                    table_product(acc3[:], lambda a: w3_w[a][:, rows].bitcast(FP8X4), lambda a: w3_sc[a][:, rows], cols, True)
                    nc.scalar.activation(out=spectral[c][:, cols], in_=acc3[:], func=ACT.Identity, bias=bias_sb[:, c : c + 1])

        for t in range(PACK):
            h = new_columns(t)
            put(t, h)
            if t + 2 < PACK:
                fetch_before(t + 2)
            if t == 1:
                quantise_w3()
                spectral_scores()
            if t + 1 < PACK:
                fetch_after(t, 0, S)

        out_rows = out.rearrange("(c p) j -> p c j", p=P)
        starts = [sum(CHUNKS[:i]) for i in range(len(CHUNKS))]
        x_w, x_sc = {}, {}

        def quantise_x(i):
            j0, width = starts[i], CHUNKS[i]
            fetch_after(PACK - 1, j0, width)
            grouped = shared([P, PACK * width], BF16, f"x_grouped{i}", f"x_grouped{i}")
            nc.scalar.copy(
                out=grouped[:].rearrange("p (c i t) -> p c t i", i=4, t=PACK),
                in_=x[:, :, j0 : j0 + width].rearrange("p t (c i) -> p c t i", i=4),
            )
            x_w[i] = held([P, width], U32, f"x_w{i}")
            x_sc[i] = held([P, width], U8, f"x_sc{i}")
            nc.vector.quantize_mx(out=x_w[i][:].bitcast(FP8X4), scales=x_sc[i][:], in_=grouped[:])

        def score(i):
            width = CHUNKS[i]
            cols = slice(starts[i], starts[i] + width)
            result = shared([P, N_TILES, width], F32, f"result{i}", f"x_grouped{i + 1}")
            for c in range(N_TILES):
                rows = slice(P * c, P * (c + 1))
                acc4 = psum.tile([P, width], F32, name="acc4", tag=("acc3", "acc2")[i % 2], bufs=3)
                nc.tensor.matmul_mx(
                    out=acc4[:],
                    lhsT=w4_w[:, rows].bitcast(FP8X4),
                    lhsT_scale=w4_sc[:, rows],
                    rhs=x_w[i][:].bitcast(FP8X4),
                    rhs_scale=x_sc[i][:],
                    start=True,
                    stop=True,
                )
                nc.vector.scalar_tensor_tensor(
                    out=result[:, c, :], in0=acc4[:], scalar=bias_sb[:, c : c + 1], in1=spectral[c][:, cols], op0=ALU.add, op1=ALU.max
                )
            nc.sync.dma_start(out=out_rows[:, :, cols], in_=result[:])

        quantise_x(0)
        for i in range(len(CHUNKS)):
            if i + 1 < len(CHUNKS):
                quantise_x(i + 1)
            score(i)
